import numpy as np
import ml_dtypes


def mxq(x, axis, fmt="e4m3"):
    dtype, down = {"e4m3": (ml_dtypes.float8_e4m3fn, 7), "e5m2": (ml_dtypes.float8_e5m2, 14)}[fmt]
    v = np.moveaxis(np.asarray(x, np.float32).astype(ml_dtypes.bfloat16).astype(np.float64), axis, -1)
    blocks = v.reshape(v.shape[:-1] + (-1, 32))
    amax = np.abs(blocks).max(-1, keepdims=True)
    byte = np.maximum(np.where(amax > 0, np.frexp(amax)[1] - 1 + 127, 0) - down, 1)
    scale = np.exp2(byte - 127.0)
    codes = (blocks / scale).astype(np.float32).astype(dtype).astype(np.float64)
    return np.moveaxis((codes * scale).reshape(v.shape), -1, axis)


WIDE = False


def mx_kscale(k):
    if not WIDE:
        return np.ones(k)
    levels = np.array([10, -10, 5, -5, 0])
    if k % 512:
        return np.exp2(np.random.permutation(np.resize(levels, k // 32))).repeat(32)
    a = np.empty((k // 512, 16))
    for p in range(k // 512):
        a[p, :8] = np.random.permutation(np.resize(levels, 8))
        for g in range(8):
            far = levels[np.abs(levels - a[p, g]) >= 10]
            a[p, g + 8] = far[np.random.randint(len(far))]
    return np.exp2(a.ravel()).repeat(32)


def f64(x):
    return np.asarray(x).astype(np.float64)


def striped(idx):
    return np.tile(idx.reshape(-1, 16).T, (8, 1)).astype(np.uint16)


def unstriped(offs):
    return offs[:16].T.reshape(-1).astype(np.int64)


def striped8(idx):
    return np.concatenate([x.reshape(-1, 16).T for x in idx]).astype(np.uint16)


def runs(offs, k):
    lists = np.stack([offs[16 * r : 16 * r + 16].T.reshape(-1) for r in range(8)]).astype(np.int64)
    return lists[np.arange(k) % 512 // 64]


def pack_weight(w):
    k, n = w.shape
    w = f64(np.asarray(w, np.float32).astype(ml_dtypes.bfloat16)).reshape(k // 32, 32, n)
    amax = np.abs(w).max(1)
    byte = np.clip(np.where(amax > 0, np.frexp(amax)[1] - 1 + 127 - 7, 1), 1, 254)
    scaled = (w * np.exp2(127.0 - byte)[:, None, :]).reshape(k, n).astype(np.float32)
    words = np.ascontiguousarray(scaled.reshape(k // 512, 128, 4, n).transpose(0, 1, 3, 2)).astype(ml_dtypes.float8_e4m3fn).view(np.uint8)
    return words, np.ascontiguousarray(byte.astype(np.uint8).reshape(k // 512, 16, n))


def unpack_weight(words, scales):
    g, p, n, _ = words.shape
    vals = np.ascontiguousarray(words).view(ml_dtypes.float8_e4m3fn).astype(np.float64) * np.repeat(np.exp2(scales.astype(np.float64) - 127.0), 8, axis=1)[..., None]
    return vals.transpose(0, 1, 3, 2).reshape(g * 512, n)


def relu(v):
    return np.maximum(v, 0.0)


K, T, S, N, H = 512, 2048, 512, 512, 512


def setup_inputs():
    n = np.random.standard_normal
    s = mx_kscale(K)[:, None]
    u = mx_kscale(H)
    packed_xT = pack_weight(n((K, T)) * s)
    return {
        "x_words": packed_xT[0],
        "x_scales": packed_xT[1],
        "w1": (n((K, H)) / np.sqrt(K) / s).astype(np.float32),
        "gn": (np.random.uniform(0.5, 1.5, (H, 1)) * u[:, None]).astype(np.float32),
        "w2": (n((H, N)) / np.sqrt(H) / u[:, None]).astype(np.float32),
        "res": (2 * n((N, S))).astype(np.float32),
        "offs": striped(np.random.permutation(T)[:S]),
        "p1": striped8(np.stack([np.random.permutation(S) for _ in range(8)])),
        "p2": striped8(np.stack([np.random.permutation(S) for _ in range(8)])),
    }


def reference(x_words, x_scales, w1, gn, w2, res, offs, p1, p2):
    xq = unpack_weight(x_words, x_scales)[:, unstriped(offs)]
    y = mxq(f64(w1), 0, "e4m3").T @ xq
    ab = np.abs(y)
    env = np.maximum(np.maximum(ab, 0.75 * (ab[np.arange(H)[:, None], runs(p1, H)])), 0.5 * (ab[np.arange(H)[:, None], runs(p2, H)]))
    z = f64(gn) * (y / (relu(env + -0.5) + 1))
    return f64(res) + (mxq(f64(w2), 0, "e4m3").T @ mxq(z, 0, "e4m3"))

@@ -1,0 +1,174 @@
+from contextlib import ExitStack
+
+import concourse.mybir as mybir
+
+K, T, S, N, H = 512, 2048, 512, 512, 512
+FLOPS = 2 * K * H * S + 2 * H * N * S
+
+F32 = mybir.dt.float32
+BF16 = mybir.dt.bfloat16
+I32 = mybir.dt.int32
+U32 = mybir.dt.uint32
+U16 = mybir.dt.uint16
+U8 = mybir.dt.uint8
+FP8X4 = mybir.dt.float8_e4m3fn_x4
+ACT = mybir.ActivationFunctionType
+ALU = mybir.AluOpType
+
+P = 128
+PACK = 4
+HALF = S // 2
+PIECE = 128
+GROUP = 2
+VEC_GATHERS = 7
+VEC_WEAVES = (0, 2)
+LAG_MAX, LAG_RECIP, LAG_MUL, LAG_OUT = 2, 4, 5, 7
+W2_STEP = 4
+RING = 9
+
+
+def tile_picked_compress8_none_p_kernel(tc, x_words, x_scales, w1, gn, w2, res, offs, p1, p2, out):
+    nc = tc.nc
+    with ExitStack() as ctx:
+        keep = ctx.enter_context(tc.tile_pool(name="keep", bufs=1))
+        psum = ctx.enter_context(tc.psum_pool(name="psum", bufs=1))
+
+        offs_sb = keep.tile([P, S // 16], U16, name="offs_sb")
+        p1_sb = keep.tile([P, S // 16], U16, name="p1_sb")
+        p2_sb = keep.tile([P, S // 16], U16, name="p2_sb")
+        w1_raw = keep.tile([P, PACK, H], F32, name="w1_raw", tag="raw")
+        gn_sb = keep.tile([P, PACK], F32, name="gn_sb")
+        x_all = keep.tile([P, T], I32, name="x_all")
+        xs_all = keep.tile([P, T], U8, name="xs_all")
+
+        nc.gpsimd.memset(xs_all[:].bitcast(I32), 0)
+        nc.sync.dma_start(out=offs_sb[:], in_=offs)
+        nc.sync.dma_start(out=w1_raw[:], in_=w1.rearrange("(p j) c -> p j c", j=PACK))
+        nc.sync.dma_start(out=x_all[:], in_=x_words[0].rearrange("p n t -> p (n t)").bitcast(I32))
+        for q in range(4):
+            nc.scalar.dma_start(out=xs_all[32 * q : 32 * q + 4, :].bitcast(I32), in_=x_scales[0, 4 * q : 4 * q + 4, :].bitcast(I32))
+        nc.sync.dma_start(out=p1_sb[:], in_=p1)
+        nc.sync.dma_start(out=p2_sb[:], in_=p2)
+        nc.gpsimd.dma_start(out=gn_sb[:], in_=gn.rearrange("(p t) o -> p (t o)", t=PACK))
+
+        warm_in = keep.tile([P, 1], F32, name="warm_in")
+        warm_out = keep.tile([P, 1], F32, name="warm_out")
+        nc.vector.memset(warm_in[:], 1.0)
+        nc.scalar.activation(out=warm_out[:], in_=warm_in[:], func=ACT.Abs_reciprocal_sqrt)
+
+        xs_pick = keep.tile([P, S], U8, name="xs_pick", align_bytes=64)
+        nc.vector.tensor_copy(out=xs_pick[:], in_=xs_all[:].indirect(offs_sb[:]))
+
+        w1_bf = keep.tile([P, H * PACK], BF16, name="w1_bf", tag="late", align_bytes=64)
+        dst = w1_bf[:].rearrange("p (t m j) -> p m j t", t=PACK, j=PACK)
+        src = w1_raw[:].rearrange("p j (m t) -> p m j t", t=PACK)
+        nc.vector.tensor_copy(out=dst[:, : 64], in_=src[:, : 64])
+        nc.scalar.copy(out=dst[:, 64 :], in_=src[:, 64 :])
+        w1_codes = keep.tile([P, H], U32, name="w1_codes", align_bytes=64)
+        w1_scales = keep.tile([P, H], U8, name="w1_scales", align_bytes=64)
+        nc.vector.quantize_mx(out=w1_codes[:].bitcast(FP8X4), scales=w1_scales[:], in_=w1_bf[:])
+
+        w2_raw = keep.tile([P, PACK, N], F32, name="w2_raw", tag="raw")
+        nc.sync.dma_start(out=w2_raw[:], in_=w2.rearrange("(p j) c -> p j c", j=PACK))
+        res_sb = keep.tile([P, PACK, S], F32, name="res_sb", tag="late", align_bytes=64)
+        nc.sync.dma_start(out=res_sb[:], in_=res.rearrange("(b p) s -> p b s", p=P))
+
+        x_pick = [keep.tile([P, HALF], U32, name=f"x_pick{h}", align_bytes=64) for h in range(2)]
+        for h in range(2):
+            nc.vector.tensor_copy(out=x_pick[h][:], in_=x_all[:].bitcast(U32).indirect(offs_sb[:, h * HALF // 16 : (h + 1) * HALF // 16]))
+
+        y = [psum.tile([P, S], F32, name=f"y{t}") for t in range(PACK)]
+        ab = [keep.tile([P, S], F32, name=f"ab{t}") for t in range(PACK)]
+        for t0 in range(0, PACK, 2):
+            for h in range(2):
+                for t in (t0, t0 + 1):
+                    cols = slice(P * t, P * (t + 1))
+                    span = slice(h * HALF, (h + 1) * HALF)
+                    nc.tensor.matmul_mx(out=y[t][:, span], lhsT=w1_codes[:, cols].bitcast(FP8X4), lhsT_scale=w1_scales[:, cols],
+                                        rhs=x_pick[h][:].bitcast(FP8X4), rhs_scale=xs_pick[:, span], start=True, stop=True)
+                    nc.scalar.activation(out=ab[t][:, span], in_=y[t][:, span], func=ACT.Abs)
+
+        w2_bf = keep.tile([P, N * PACK], BF16, name="w2_bf", align_bytes=64)
+        w2_codes = keep.tile([P, N], U32, name="w2_codes", align_bytes=64)
+        w2_scales = keep.tile([P, N], U8, name="w2_scales", align_bytes=64)
+
+        def prepare_w2():
+            nc.gpsimd.tensor_scalar(out=w2_bf[:].rearrange("p (c j) -> p c j", j=PACK), in0=w2_raw[:].rearrange("p j c -> p c j"),
+                                    scalar1=1.0, scalar2=0.0, op0=ALU.mult, op1=ALU.add)
+            nc.vector.quantize_mx(out=w2_codes[:].bitcast(FP8X4), scales=w2_scales[:], in_=w2_bf[:])
+
+        units = [(h, t0) for h in range(2) for t0 in range(0, PACK, GROUP)]
+        near, far, den, rec, acc = {}, {}, {}, {}, {}
+        zt = [keep.tile([P, PACK, HALF], BF16, name=f"zt{h}") for h in range(2)]
+
+        def gathers(u):
+            h, t0 = units[u]
+            lcols = slice(h * HALF // 16, (h + 1) * HALF // 16)
+            near[u] = keep.tile([P, GROUP, HALF], F32, name=f"near{u}", tag=f"a{u % RING}")
+            far[u] = keep.tile([P, GROUP, HALF], F32, name=f"far{u}", tag=f"b{u % RING}")
+            for i in range(GROUP):
+                for k, (dst_g, lst, factor) in enumerate(((near[u], p1_sb, 0.75), (far[u], p2_sb, 0.5))):
+                    window = ab[t0 + i][:].indirect(lst[:, lcols])
+                    if 2 * (u * GROUP + i) + k < VEC_GATHERS:
+                        nc.vector.tensor_scalar(out=dst_g[:, i, :], in0=window, scalar1=factor, scalar2=0.5, op0=ALU.mult, op1=ALU.add)
+                    else:
+                        nc.scalar.activation(out=dst_g[:, i, :], in_=window, func=ACT.Copy, scale=factor, bias=0.5)
+
+        def largest(u):
+            h, t0 = units[u]
+            span = slice(h * HALF, (h + 1) * HALF)
+            both = keep.tile([P, GROUP, HALF], F32, name=f"both{u}")
+            nc.vector.scalar_tensor_tensor(out=both[:], in0=far[u][:], scalar=1.0, in1=near[u][:], op0=ALU.max, op1=ALU.max)
+            den[u] = keep.tile([P, GROUP, HALF], F32, name=f"den{u}", tag=f"a{u % RING}")
+            for i in range(GROUP):
+                nc.vector.scalar_tensor_tensor(out=den[u][:, i, :], in0=ab[t0 + i][:, span], scalar=0.5, in1=both[:, i, :], op0=ALU.add, op1=ALU.max)
+
+        def recip(u):
+            sq = keep.tile([P, GROUP, HALF], F32, name=f"sq{u}", tag=f"b{u % RING}")
+            rec[u] = keep.tile([P, GROUP, HALF], F32, name=f"rec{u}")
+            nc.scalar.activation(out=sq[:], in_=den[u][:], func=ACT.Square)
+            nc.scalar.activation(out=rec[u][:], in_=sq[:], func=ACT.Abs_reciprocal_sqrt)
+
+        def multiply(u):
+            h, t0 = units[u]
+            span = slice(h * HALF, (h + 1) * HALF)
+            for i in range(GROUP):
+                t = t0 + i
+                nc.vector.scalar_tensor_tensor(out=zt[h][:, t, :], in0=y[t][:, span], scalar=gn_sb[:, t : t + 1], in1=rec[u][:, i, :], op0=ALU.mult, op1=ALU.mult)
+            if t0 + GROUP == PACK:
+                pieces = range(h * HALF // PIECE, (h + 1) * HALF // PIECE)
+                woven = {}
+                for c in pieces:
+                    woven[c] = keep.tile([P, PIECE * PACK], BF16, name=f"zi{c}", align_bytes=64)
+                    s0 = c * PIECE - h * HALF
+                    to = woven[c][:].rearrange("p (c i t) -> p c t i", i=4, t=PACK)
+                    fro = zt[h][:, :, s0 : s0 + PIECE].rearrange("p t (c i) -> p c t i", i=4)
+                    if c in VEC_WEAVES:
+                        nc.vector.tensor_copy(out=to, in_=fro)
+                    else:
+                        nc.scalar.copy(out=to, in_=fro)
+                for c in pieces:
+                    z_codes = keep.tile([P, PIECE], U32, name=f"zc{c}", align_bytes=64)
+                    z_scales = keep.tile([P, PIECE], U8, name=f"zs{c}", align_bytes=64)
+                    nc.vector.quantize_mx(out=z_codes[:].bitcast(FP8X4), scales=z_scales[:], in_=woven[c][:])
+                    acc[c] = psum.tile([P, PACK, PIECE], F32, name=f"acc{c}")
+                    for b in range(PACK):
+                        cols = slice(P * b, P * (b + 1))
+                        nc.tensor.matmul_mx(out=acc[c][:, b, :], lhsT=w2_codes[:, cols].bitcast(FP8X4), lhsT_scale=w2_scales[:, cols],
+                                            rhs=z_codes[:].bitcast(FP8X4), rhs_scale=z_scales[:], start=True, stop=True)
+
+        def finish(u):
+            h, t0 = units[u]
+            if t0 + GROUP == PACK:
+                for c in range(h * HALF // PIECE, (h + 1) * HALF // PIECE):
+                    span = slice(c * PIECE, (c + 1) * PIECE)
+                    o_sb = keep.tile([P, PACK, PIECE], F32, name=f"o{c}")
+                    nc.vector.tensor_tensor(out=o_sb[:], in0=acc[c][:], in1=res_sb[:, :, span], op=ALU.add)
+                    nc.sync.dma_start(out=out.rearrange("(b p) s -> p b s", p=P)[:, :, span], in_=o_sb[:])
+
+        for step in range(len(units) + LAG_OUT):
+            for lag, stage in ((LAG_RECIP, recip), (0, gathers), (LAG_MAX, largest), (LAG_MUL, multiply), (LAG_OUT, finish)):
+                if 0 <= step - lag < len(units):
+                    stage(step - lag)
+            if step == W2_STEP:
+                prepare_w2()

@@ -21,9 +21,11 @@ HALF = S // 2
 PIECE = 128
 GROUP = 2
 VEC_GATHERS = 7
-VEC_WEAVES = (0, 2)
+VEC_WEAVES = (128, 160)
 LAG_MAX, LAG_RECIP, LAG_MUL, LAG_OUT = 2, 4, 5, 7
 W2_STEP = 4
+OUT_TILES = (2, 1)
+OUT_BANKS = ((4, 5), (6, 7, 0, 1))
 RING = 9
 
 
@@ -77,16 +79,16 @@ def tile_picked_compress8_none_p_kernel(tc, x_words, x_scales, w1, gn, w2, res, 
         for h in range(2):
             nc.vector.tensor_copy(out=x_pick[h][:], in_=x_all[:].bitcast(U32).indirect(offs_sb[:, h * HALF // 16 : (h + 1) * HALF // 16]))
 
-        y = [psum.tile([P, S], F32, name=f"y{t}") for t in range(PACK)]
+        y = {(h, i): psum.tile([P, 2, HALF], F32, name=f"y{h}{i}", tag=f"bank{2 * h + i}") for h in range(2) for i in range(GROUP)}
         ab = [keep.tile([P, S], F32, name=f"ab{t}") for t in range(PACK)]
-        for t0 in range(0, PACK, 2):
+        for t0 in range(0, PACK, GROUP):
             for h in range(2):
-                for t in (t0, t0 + 1):
-                    cols = slice(P * t, P * (t + 1))
-                    span = slice(h * HALF, (h + 1) * HALF)
-                    nc.tensor.matmul_mx(out=y[t][:, span], lhsT=w1_codes[:, cols].bitcast(FP8X4), lhsT_scale=w1_scales[:, cols],
+                span = slice(h * HALF, (h + 1) * HALF)
+                for i in range(GROUP):
+                    cols = slice(P * (t0 + i), P * (t0 + i + 1))
+                    nc.tensor.matmul_mx(out=y[h, i][:, t0 // GROUP, :], lhsT=w1_codes[:, cols].bitcast(FP8X4), lhsT_scale=w1_scales[:, cols],
                                         rhs=x_pick[h][:].bitcast(FP8X4), rhs_scale=xs_pick[:, span], start=True, stop=True)
-                    nc.scalar.activation(out=ab[t][:, span], in_=y[t][:, span], func=ACT.Abs)
+                    nc.scalar.activation(out=ab[t0 + i][:, span], in_=y[h, i][:, t0 // GROUP, :], func=ACT.Abs)
 
         w2_bf = keep.tile([P, N * PACK], BF16, name="w2_bf", align_bytes=64)
         w2_codes = keep.tile([P, N], U32, name="w2_codes", align_bytes=64)
@@ -134,37 +136,37 @@ def tile_picked_compress8_none_p_kernel(tc, x_words, x_scales, w1, gn, w2, res, 
             span = slice(h * HALF, (h + 1) * HALF)
             for i in range(GROUP):
                 t = t0 + i
-                nc.vector.scalar_tensor_tensor(out=zt[h][:, t, :], in0=y[t][:, span], scalar=gn_sb[:, t : t + 1], in1=rec[u][:, i, :], op0=ALU.mult, op1=ALU.mult)
+                nc.vector.scalar_tensor_tensor(out=zt[h][:, t, :], in0=y[h, i][:, t0 // GROUP, :], scalar=gn_sb[:, t : t + 1], in1=rec[u][:, i, :], op0=ALU.mult, op1=ALU.mult)
             if t0 + GROUP == PACK:
-                pieces = range(h * HALF // PIECE, (h + 1) * HALF // PIECE)
-                woven = {}
-                for c in pieces:
-                    woven[c] = keep.tile([P, PIECE * PACK], BF16, name=f"zi{c}", align_bytes=64)
-                    s0 = c * PIECE - h * HALF
-                    to = woven[c][:].rearrange("p (c i t) -> p c t i", i=4, t=PACK)
-                    fro = zt[h][:, :, s0 : s0 + PIECE].rearrange("p t (c i) -> p c t i", i=4)
-                    if c in VEC_WEAVES:
-                        nc.vector.tensor_copy(out=to, in_=fro)
-                    else:
-                        nc.scalar.copy(out=to, in_=fro)
-                for c in pieces:
-                    z_codes = keep.tile([P, PIECE], U32, name=f"zc{c}", align_bytes=64)
-                    z_scales = keep.tile([P, PIECE], U8, name=f"zs{c}", align_bytes=64)
-                    nc.vector.quantize_mx(out=z_codes[:].bitcast(FP8X4), scales=z_scales[:], in_=woven[c][:])
-                    acc[c] = psum.tile([P, PACK, PIECE], F32, name=f"acc{c}")
-                    for b in range(PACK):
-                        cols = slice(P * b, P * (b + 1))
-                        nc.tensor.matmul_mx(out=acc[c][:, b, :], lhsT=w2_codes[:, cols].bitcast(FP8X4), lhsT_scale=w2_scales[:, cols],
+                woven = keep.tile([P, HALF * PACK], BF16, name=f"woven{h}", align_bytes=64)
+                to = woven[:].rearrange("p (c i t) -> p c t i", i=4, t=PACK)
+                fro = zt[h][:].rearrange("p t (c i) -> p c t i", i=4)
+                cut = VEC_WEAVES[h] // 4
+                if cut > 0:
+                    nc.vector.tensor_copy(out=to[:, :cut], in_=fro[:, :cut])
+                if cut < HALF // 4:
+                    nc.scalar.copy(out=to[:, cut:], in_=fro[:, cut:])
+                z_codes = keep.tile([P, HALF], U32, name=f"zc{h}", align_bytes=64)
+                z_scales = keep.tile([P, HALF], U8, name=f"zs{h}", align_bytes=64)
+                nc.vector.quantize_mx(out=z_codes[:].bitcast(FP8X4), scales=z_scales[:], in_=woven[:])
+                per_bank = OUT_TILES[h]
+                for b0 in range(0, PACK, per_bank):
+                    acc[h, b0] = psum.tile([P, per_bank, HALF], F32, name=f"acc{h}{b0}", tag=f"bank{OUT_BANKS[h][b0 // per_bank]}")
+                    for i in range(per_bank):
+                        cols = slice(P * (b0 + i), P * (b0 + i + 1))
+                        nc.tensor.matmul_mx(out=acc[h, b0][:, i, :], lhsT=w2_codes[:, cols].bitcast(FP8X4), lhsT_scale=w2_scales[:, cols],
                                             rhs=z_codes[:].bitcast(FP8X4), rhs_scale=z_scales[:], start=True, stop=True)
 
         def finish(u):
             h, t0 = units[u]
             if t0 + GROUP == PACK:
-                for c in range(h * HALF // PIECE, (h + 1) * HALF // PIECE):
-                    span = slice(c * PIECE, (c + 1) * PIECE)
-                    o_sb = keep.tile([P, PACK, PIECE], F32, name=f"o{c}")
-                    nc.vector.tensor_tensor(out=o_sb[:], in0=acc[c][:], in1=res_sb[:, :, span], op=ALU.add)
-                    nc.sync.dma_start(out=out.rearrange("(b p) s -> p b s", p=P)[:, :, span], in_=o_sb[:])
+                span = slice(h * HALF, (h + 1) * HALF)
+                per_bank = OUT_TILES[h]
+                for b0 in range(0, PACK, per_bank):
+                    o_sb = keep.tile([P, per_bank, HALF], F32, name=f"o{h}{b0}")
+                    nc.vector.tensor_tensor(out=o_sb[:], in0=acc[h, b0][:], in1=res_sb[:, b0 : b0 + per_bank, span], op=ALU.add)
+                    queue = nc.scalar if (h == 1 and b0 % 2 == 1) else nc.sync
+                    queue.dma_start(out=out.rearrange("(b p) s -> p b s", p=P)[:, b0 : b0 + per_bank, span], in_=o_sb[:])
 
         for step in range(len(units) + LAG_OUT):
             for lag, stage in ((LAG_RECIP, recip), (0, gathers), (LAG_MAX, largest), (LAG_MUL, multiply), (LAG_OUT, finish)):

from contextlib import ExitStack

import concourse.mybir as mybir

K, T, S, N, H = 512, 2048, 512, 512, 512
FLOPS = 2 * K * H * S + 2 * H * N * S

F32 = mybir.dt.float32
BF16 = mybir.dt.bfloat16
I32 = mybir.dt.int32
U32 = mybir.dt.uint32
U16 = mybir.dt.uint16
U8 = mybir.dt.uint8
FP8X4 = mybir.dt.float8_e4m3fn_x4
ACT = mybir.ActivationFunctionType
ALU = mybir.AluOpType

P = 128
PACK = 4
HALF = S // 2
PIECE = 128
GROUP = 2
VEC_GATHERS = 7
VEC_WEAVES = (128, 160)
LAG_MAX, LAG_RECIP, LAG_MUL, LAG_OUT = 2, 4, 5, 7
W2_STEP = 4
OUT_TILES = (2, 1)
OUT_BANKS = ((4, 5), (6, 7, 0, 1))
RING = 9


def tile_picked_compress8_none_p_kernel(tc, x_words, x_scales, w1, gn, w2, res, offs, p1, p2, out):
    nc = tc.nc
    with ExitStack() as ctx:
        keep = ctx.enter_context(tc.tile_pool(name="keep", bufs=1))
        psum = ctx.enter_context(tc.psum_pool(name="psum", bufs=1))

        offs_sb = keep.tile([P, S // 16], U16, name="offs_sb")
        p1_sb = keep.tile([P, S // 16], U16, name="p1_sb")
        p2_sb = keep.tile([P, S // 16], U16, name="p2_sb")
        w1_raw = keep.tile([P, PACK, H], F32, name="w1_raw", tag="raw")
        gn_sb = keep.tile([P, PACK], F32, name="gn_sb")
        x_all = keep.tile([P, T], I32, name="x_all")
        xs_all = keep.tile([P, T], U8, name="xs_all")

        nc.gpsimd.memset(xs_all[:].bitcast(I32), 0)
        nc.sync.dma_start(out=offs_sb[:], in_=offs)
        nc.sync.dma_start(out=w1_raw[:], in_=w1.rearrange("(p j) c -> p j c", j=PACK))
        nc.sync.dma_start(out=x_all[:], in_=x_words[0].rearrange("p n t -> p (n t)").bitcast(I32))
        for q in range(4):
            nc.scalar.dma_start(out=xs_all[32 * q : 32 * q + 4, :].bitcast(I32), in_=x_scales[0, 4 * q : 4 * q + 4, :].bitcast(I32))
        nc.sync.dma_start(out=p1_sb[:], in_=p1)
        nc.sync.dma_start(out=p2_sb[:], in_=p2)
        nc.gpsimd.dma_start(out=gn_sb[:], in_=gn.rearrange("(p t) o -> p (t o)", t=PACK))

        warm_in = keep.tile([P, 1], F32, name="warm_in")
        warm_out = keep.tile([P, 1], F32, name="warm_out")
        nc.vector.memset(warm_in[:], 1.0)
        nc.scalar.activation(out=warm_out[:], in_=warm_in[:], func=ACT.Abs_reciprocal_sqrt)

        xs_pick = keep.tile([P, S], U8, name="xs_pick", align_bytes=64)
        nc.vector.tensor_copy(out=xs_pick[:], in_=xs_all[:].indirect(offs_sb[:]))

        w1_bf = keep.tile([P, H * PACK], BF16, name="w1_bf", tag="late", align_bytes=64)
        dst = w1_bf[:].rearrange("p (t m j) -> p m j t", t=PACK, j=PACK)
        src = w1_raw[:].rearrange("p j (m t) -> p m j t", t=PACK)
        nc.vector.tensor_copy(out=dst[:, : 64], in_=src[:, : 64])
        nc.scalar.copy(out=dst[:, 64 :], in_=src[:, 64 :])
        w1_codes = keep.tile([P, H], U32, name="w1_codes", align_bytes=64)
        w1_scales = keep.tile([P, H], U8, name="w1_scales", align_bytes=64)
        nc.vector.quantize_mx(out=w1_codes[:].bitcast(FP8X4), scales=w1_scales[:], in_=w1_bf[:])

        w2_raw = keep.tile([P, PACK, N], F32, name="w2_raw", tag="raw")
        nc.sync.dma_start(out=w2_raw[:], in_=w2.rearrange("(p j) c -> p j c", j=PACK))
        res_sb = keep.tile([P, PACK, S], F32, name="res_sb", tag="late", align_bytes=64)
        nc.sync.dma_start(out=res_sb[:], in_=res.rearrange("(b p) s -> p b s", p=P))

        x_pick = [keep.tile([P, HALF], U32, name=f"x_pick{h}", align_bytes=64) for h in range(2)]
        for h in range(2):
            nc.vector.tensor_copy(out=x_pick[h][:], in_=x_all[:].bitcast(U32).indirect(offs_sb[:, h * HALF // 16 : (h + 1) * HALF // 16]))

        y = {(h, i): psum.tile([P, 2, HALF], F32, name=f"y{h}{i}", tag=f"bank{2 * h + i}") for h in range(2) for i in range(GROUP)}
        ab = [keep.tile([P, S], F32, name=f"ab{t}") for t in range(PACK)]
        for t0 in range(0, PACK, GROUP):
            for h in range(2):
                span = slice(h * HALF, (h + 1) * HALF)
                for i in range(GROUP):
                    cols = slice(P * (t0 + i), P * (t0 + i + 1))
                    nc.tensor.matmul_mx(out=y[h, i][:, t0 // GROUP, :], lhsT=w1_codes[:, cols].bitcast(FP8X4), lhsT_scale=w1_scales[:, cols],
                                        rhs=x_pick[h][:].bitcast(FP8X4), rhs_scale=xs_pick[:, span], start=True, stop=True)
                    nc.scalar.activation(out=ab[t0 + i][:, span], in_=y[h, i][:, t0 // GROUP, :], func=ACT.Abs)

        w2_bf = keep.tile([P, N * PACK], BF16, name="w2_bf", align_bytes=64)
        w2_codes = keep.tile([P, N], U32, name="w2_codes", align_bytes=64)
        w2_scales = keep.tile([P, N], U8, name="w2_scales", align_bytes=64)

        def prepare_w2():
            nc.gpsimd.tensor_scalar(out=w2_bf[:].rearrange("p (c j) -> p c j", j=PACK), in0=w2_raw[:].rearrange("p j c -> p c j"),
                                    scalar1=1.0, scalar2=0.0, op0=ALU.mult, op1=ALU.add)
            nc.vector.quantize_mx(out=w2_codes[:].bitcast(FP8X4), scales=w2_scales[:], in_=w2_bf[:])

        units = [(h, t0) for h in range(2) for t0 in range(0, PACK, GROUP)]
        near, far, den, rec, acc = {}, {}, {}, {}, {}
        zt = [keep.tile([P, PACK, HALF], BF16, name=f"zt{h}") for h in range(2)]

        def gathers(u):
            h, t0 = units[u]
            lcols = slice(h * HALF // 16, (h + 1) * HALF // 16)
            near[u] = keep.tile([P, GROUP, HALF], F32, name=f"near{u}", tag=f"a{u % RING}")
            far[u] = keep.tile([P, GROUP, HALF], F32, name=f"far{u}", tag=f"b{u % RING}")
            for i in range(GROUP):
                for k, (dst_g, lst, factor) in enumerate(((near[u], p1_sb, 0.75), (far[u], p2_sb, 0.5))):
                    window = ab[t0 + i][:].indirect(lst[:, lcols])
                    if 2 * (u * GROUP + i) + k < VEC_GATHERS:
                        nc.vector.tensor_scalar(out=dst_g[:, i, :], in0=window, scalar1=factor, scalar2=0.5, op0=ALU.mult, op1=ALU.add)
                    else:
                        nc.scalar.activation(out=dst_g[:, i, :], in_=window, func=ACT.Copy, scale=factor, bias=0.5)

        def largest(u):
            h, t0 = units[u]
            span = slice(h * HALF, (h + 1) * HALF)
            both = keep.tile([P, GROUP, HALF], F32, name=f"both{u}")
            nc.vector.scalar_tensor_tensor(out=both[:], in0=far[u][:], scalar=1.0, in1=near[u][:], op0=ALU.max, op1=ALU.max)
            den[u] = keep.tile([P, GROUP, HALF], F32, name=f"den{u}", tag=f"a{u % RING}")
            for i in range(GROUP):
                nc.vector.scalar_tensor_tensor(out=den[u][:, i, :], in0=ab[t0 + i][:, span], scalar=0.5, in1=both[:, i, :], op0=ALU.add, op1=ALU.max)

        def recip(u):
            sq = keep.tile([P, GROUP, HALF], F32, name=f"sq{u}", tag=f"b{u % RING}")
            rec[u] = keep.tile([P, GROUP, HALF], F32, name=f"rec{u}")
            nc.scalar.activation(out=sq[:], in_=den[u][:], func=ACT.Square)
            nc.scalar.activation(out=rec[u][:], in_=sq[:], func=ACT.Abs_reciprocal_sqrt)

        def multiply(u):
            h, t0 = units[u]
            span = slice(h * HALF, (h + 1) * HALF)
            for i in range(GROUP):
                t = t0 + i
                nc.vector.scalar_tensor_tensor(out=zt[h][:, t, :], in0=y[h, i][:, t0 // GROUP, :], scalar=gn_sb[:, t : t + 1], in1=rec[u][:, i, :], op0=ALU.mult, op1=ALU.mult)
            if t0 + GROUP == PACK:
                woven = keep.tile([P, HALF * PACK], BF16, name=f"woven{h}", align_bytes=64)
                to = woven[:].rearrange("p (c i t) -> p c t i", i=4, t=PACK)
                fro = zt[h][:].rearrange("p t (c i) -> p c t i", i=4)
                cut = VEC_WEAVES[h] // 4
                if cut > 0:
                    nc.vector.tensor_copy(out=to[:, :cut], in_=fro[:, :cut])
                if cut < HALF // 4:
                    nc.scalar.copy(out=to[:, cut:], in_=fro[:, cut:])
                z_codes = keep.tile([P, HALF], U32, name=f"zc{h}", align_bytes=64)
                z_scales = keep.tile([P, HALF], U8, name=f"zs{h}", align_bytes=64)
                nc.vector.quantize_mx(out=z_codes[:].bitcast(FP8X4), scales=z_scales[:], in_=woven[:])
                per_bank = OUT_TILES[h]
                for b0 in range(0, PACK, per_bank):
                    acc[h, b0] = psum.tile([P, per_bank, HALF], F32, name=f"acc{h}{b0}", tag=f"bank{OUT_BANKS[h][b0 // per_bank]}")
                    for i in range(per_bank):
                        cols = slice(P * (b0 + i), P * (b0 + i + 1))
                        nc.tensor.matmul_mx(out=acc[h, b0][:, i, :], lhsT=w2_codes[:, cols].bitcast(FP8X4), lhsT_scale=w2_scales[:, cols],
                                            rhs=z_codes[:].bitcast(FP8X4), rhs_scale=z_scales[:], start=True, stop=True)

        def finish(u):
            h, t0 = units[u]
            if t0 + GROUP == PACK:
                span = slice(h * HALF, (h + 1) * HALF)
                per_bank = OUT_TILES[h]
                for b0 in range(0, PACK, per_bank):
                    o_sb = keep.tile([P, per_bank, HALF], F32, name=f"o{h}{b0}")
                    nc.vector.tensor_tensor(out=o_sb[:], in0=acc[h, b0][:], in1=res_sb[:, b0 : b0 + per_bank, span], op=ALU.add)
                    queue = nc.scalar if (h == 1 and b0 % 2 == 1) else nc.sync
                    queue.dma_start(out=out.rearrange("(b p) s -> p b s", p=P)[:, b0 : b0 + per_bank, span], in_=o_sb[:])

        for step in range(len(units) + LAG_OUT):
            for lag, stage in ((LAG_RECIP, recip), (0, gathers), (LAG_MAX, largest), (LAG_MUL, multiply), (LAG_OUT, finish)):
                if 0 <= step - lag < len(units):
                    stage(step - lag)
            if step == W2_STEP:
                prepare_w2()
